import numpy as np
import ml_dtypes

BF16 = ml_dtypes.bfloat16


def bf(x):
    return np.asarray(x, np.float32).astype(BF16)


def f32(x):
    return np.asarray(x, np.float32)


def f64(x):
    return np.asarray(x).astype(np.float64)


def striped(idx):
    return np.concatenate([l.reshape(-1, 16).T for l in idx])


def rows(idx, k):
    return np.tile(np.repeat(idx, 16, axis=0), (k // (16 * 8), 1))


def look(tab, idx):
    return np.take_along_axis(f64(tab), rows(idx, len(tab)), axis=1)


K, S, V, N, M = 256, 2048, 1536, 1536, 256


def setup_inputs():
    return {"tab": f32(np.random.standard_normal((K, S))), "y": f32(np.random.standard_normal((K, V))), "w": bf(np.random.standard_normal((K, M)) / np.sqrt(K)), "b": f32(0.5 * np.random.standard_normal((M, 1))), "offs": striped(np.stack([np.random.permutation(S)[:N] for _ in range(8)]))}


def reference(tab, y, w, b, offs):
    idx = np.stack([g.T.reshape(-1) for g in np.split(offs, 8)])
    t = look(tab, idx)
    x = np.maximum(t, 0.0) * f64(y)
    y = f64(w).T @ x
    return np.maximum(y + f64(b), 0.0)

@@ -1,0 +1,77 @@
+import concourse.mybir as mybir
+
+F32 = mybir.dt.float32
+BF16 = mybir.dt.bfloat16
+U16 = mybir.dt.uint16
+RELU = mybir.ActivationFunctionType.Relu
+ADD = mybir.AluOpType.add
+MAX = mybir.AluOpType.max
+MULT = mybir.AluOpType.mult
+
+P = 128
+K_ROWS = 256
+M_ROWS = 256
+TABLE_COLS = 2048
+N = 1536
+PIECE = 512
+K_BLOCKS = K_ROWS // P
+M_BLOCKS = M_ROWS // P
+N_PIECES = N // PIECE
+OFFSET_COLS = PIECE // 16
+
+FLOPS = 2 * K_ROWS * M_ROWS * N
+
+
+def tile_lookup_gate_relu_relu_kernel(tc, tab, y, w, b, offs, out):
+    nc = tc.nc
+    with (
+        tc.tile_pool(name="held", bufs=1) as held,
+        tc.tile_pool(name="work", bufs=K_BLOCKS * N_PIECES) as work,
+        tc.psum_pool(name="psum", bufs=M_BLOCKS * N_PIECES) as psum,
+    ):
+        offsets = held.tile([P, N // 16], U16, name="offsets")
+        nc.sync.dma_start(offsets[:], offs)
+        tables = []
+        for k in range(K_BLOCKS):
+            table = held.tile([P, TABLE_COLS], F32, name=f"table{k}")
+            nc.sync.dma_start(table[:], tab[k * P : (k + 1) * P, :])
+            tables.append(table)
+        weights = held.tile([P, K_BLOCKS, M_ROWS], BF16, name="weights")
+        nc.sync.dma_start(weights[:], w.rearrange("(k p) m -> p k m", p=P))
+        streams = []
+        for j in range(N_PIECES):
+            stream = held.tile([P, K_BLOCKS, PIECE], F32, name=f"stream{j}")
+            y_piece = y[:, j * PIECE : (j + 1) * PIECE]
+            nc.sync.dma_start(stream[:], y_piece.rearrange("(k p) v -> p k v", p=P))
+            streams.append(stream)
+        biases = []
+        for m in range(M_BLOCKS):
+            bias = held.tile([P, 1], F32, name=f"bias{m}")
+            nc.sync.dma_start(bias[:], b[m * P : (m + 1) * P, :])
+            biases.append(bias)
+
+        for j in range(N_PIECES):
+            cols = slice(j * PIECE, (j + 1) * PIECE)
+            piece_offsets = offsets[:, j * OFFSET_COLS : (j + 1) * OFFSET_COLS]
+
+            xs = []
+            for k in range(K_BLOCKS):
+                gate = work.tile([P, PIECE], F32, name="gate")
+                nc.scalar.activation(gate[:], tables[k][:].indirect(piece_offsets), RELU)
+                x = work.tile([P, PIECE], BF16, name="x")
+                nc.vector.tensor_tensor(x[:], gate[:], streams[j][:, k, :], MULT)
+                xs.append(x)
+
+            for m in range(M_BLOCKS):
+                acc = psum.tile([P, PIECE], F32, name="acc")
+                for k in range(K_BLOCKS):
+                    nc.tensor.matmul(
+                        acc[:],
+                        weights[:, k, m * P : (m + 1) * P],
+                        xs[k][:],
+                        start=k == 0,
+                        stop=k == K_BLOCKS - 1,
+                    )
+                result = work.tile([P, PIECE], F32, name="result")
+                nc.vector.tensor_scalar(result[:], acc[:], biases[m][:], 0.0, ADD, MAX)
+                nc.sync.dma_start(out[m * P : (m + 1) * P, cols], result[:])

@@ -29,6 +29,11 @@ def tile_lookup_gate_relu_relu_kernel(tc, tab, y, w, b, offs, out):
         tc.tile_pool(name="work", bufs=K_BLOCKS * N_PIECES) as work,
         tc.psum_pool(name="psum", bufs=M_BLOCKS * N_PIECES) as psum,
     ):
+        zero = held.tile([P, 1], F32, name="zero")
+        nc.vector.memset(zero[:], 0.0)
+        warm = held.tile([P, 1], F32, name="warm")
+        nc.scalar.activation(warm[:], zero[:], RELU)
+
         offsets = held.tile([P, N // 16], U16, name="offsets")
         nc.sync.dma_start(offsets[:], offs)
         tables = []
@@ -38,17 +43,17 @@ def tile_lookup_gate_relu_relu_kernel(tc, tab, y, w, b, offs, out):
             tables.append(table)
         weights = held.tile([P, K_BLOCKS, M_ROWS], BF16, name="weights")
         nc.sync.dma_start(weights[:], w.rearrange("(k p) m -> p k m", p=P))
+        biases = []
+        for m in range(M_BLOCKS):
+            bias = held.tile([P, 1], F32, name=f"bias{m}")
+            nc.sync.dma_start(bias[:], b[m * P : (m + 1) * P, :])
+            biases.append(bias)
         streams = []
         for j in range(N_PIECES):
             stream = held.tile([P, K_BLOCKS, PIECE], F32, name=f"stream{j}")
             y_piece = y[:, j * PIECE : (j + 1) * PIECE]
             nc.sync.dma_start(stream[:], y_piece.rearrange("(k p) v -> p k v", p=P))
             streams.append(stream)
-        biases = []
-        for m in range(M_BLOCKS):
-            bias = held.tile([P, 1], F32, name=f"bias{m}")
-            nc.sync.dma_start(bias[:], b[m * P : (m + 1) * P, :])
-            biases.append(bias)
 
         for j in range(N_PIECES):
             cols = slice(j * PIECE, (j + 1) * PIECE)

@@ -48,35 +48,37 @@ def tile_lookup_gate_relu_relu_kernel(tc, tab, y, w, b, offs, out):
             bias = held.tile([P, 1], F32, name=f"bias{m}")
             nc.sync.dma_start(bias[:], b[m * P : (m + 1) * P, :])
             biases.append(bias)
-        streams = []
-        for j in range(N_PIECES):
-            stream = held.tile([P, K_BLOCKS, PIECE], F32, name=f"stream{j}")
-            y_piece = y[:, j * PIECE : (j + 1) * PIECE]
-            nc.sync.dma_start(stream[:], y_piece.rearrange("(k p) v -> p k v", p=P))
-            streams.append(stream)
+        streams = {}
+        for k in range(K_BLOCKS):
+            for j in range(N_PIECES):
+                stream = held.tile([P, PIECE], F32, name=f"stream{k}_{j}")
+                nc.sync.dma_start(stream[:], y[k * P : (k + 1) * P, j * PIECE : (j + 1) * PIECE])
+                streams[k, j] = stream
 
-        for j in range(N_PIECES):
-            cols = slice(j * PIECE, (j + 1) * PIECE)
-            piece_offsets = offsets[:, j * OFFSET_COLS : (j + 1) * OFFSET_COLS]
-
-            xs = []
-            for k in range(K_BLOCKS):
+        xs = {}
+        for k in range(K_BLOCKS):
+            for j in range(N_PIECES):
+                piece_offsets = offsets[:, j * OFFSET_COLS : (j + 1) * OFFSET_COLS]
                 gate = work.tile([P, PIECE], F32, name="gate")
                 nc.scalar.activation(gate[:], tables[k][:].indirect(piece_offsets), RELU)
                 x = work.tile([P, PIECE], BF16, name="x")
-                nc.vector.tensor_tensor(x[:], gate[:], streams[j][:, k, :], MULT)
-                xs.append(x)
+                nc.vector.tensor_tensor(x[:], gate[:], streams[k, j][:], MULT)
+                xs[k, j] = x
 
+        for j in range(N_PIECES):
             for m in range(M_BLOCKS):
                 acc = psum.tile([P, PIECE], F32, name="acc")
                 for k in range(K_BLOCKS):
                     nc.tensor.matmul(
                         acc[:],
                         weights[:, k, m * P : (m + 1) * P],
-                        xs[k][:],
+                        xs[k, j][:],
                         start=k == 0,
                         stop=k == K_BLOCKS - 1,
                     )
                 result = work.tile([P, PIECE], F32, name="result")
-                nc.vector.tensor_scalar(result[:], acc[:], biases[m][:], 0.0, ADD, MAX)
-                nc.sync.dma_start(out[m * P : (m + 1) * P, cols], result[:])
+                if m % 2 == 0:
+                    nc.vector.tensor_scalar(result[:], acc[:], biases[m][:], 0.0, ADD, MAX)
+                else:
+                    nc.scalar.activation(result[:], acc[:], RELU, bias=biases[m][:])
+                nc.sync.dma_start(out[m * P : (m + 1) * P, j * PIECE : (j + 1) * PIECE], result[:])

@@ -14,6 +14,7 @@ M_ROWS = 256
 TABLE_COLS = 2048
 N = 1536
 PIECE = 512
+GROUP = 2
 K_BLOCKS = K_ROWS // P
 M_BLOCKS = M_ROWS // P
 N_PIECES = N // PIECE
@@ -24,6 +25,11 @@ FLOPS = 2 * K_ROWS * M_ROWS * N
 
 def tile_lookup_gate_relu_relu_kernel(tc, tab, y, w, b, offs, out):
     nc = tc.nc
+    order = []
+    for first in range(0, N_PIECES, GROUP):
+        for k in range(K_BLOCKS):
+            for j in range(first, min(first + GROUP, N_PIECES)):
+                order.append((k, j))
     with (
         tc.tile_pool(name="held", bufs=1) as held,
         tc.tile_pool(name="work", bufs=K_BLOCKS * N_PIECES) as work,
@@ -49,21 +55,19 @@ def tile_lookup_gate_relu_relu_kernel(tc, tab, y, w, b, offs, out):
             nc.sync.dma_start(bias[:], b[m * P : (m + 1) * P, :])
             biases.append(bias)
         streams = {}
-        for k in range(K_BLOCKS):
-            for j in range(N_PIECES):
-                stream = held.tile([P, PIECE], F32, name=f"stream{k}_{j}")
-                nc.sync.dma_start(stream[:], y[k * P : (k + 1) * P, j * PIECE : (j + 1) * PIECE])
-                streams[k, j] = stream
+        for k, j in order:
+            stream = held.tile([P, PIECE], F32, name=f"stream{k}_{j}")
+            nc.sync.dma_start(stream[:], y[k * P : (k + 1) * P, j * PIECE : (j + 1) * PIECE])
+            streams[k, j] = stream
 
         xs = {}
-        for k in range(K_BLOCKS):
-            for j in range(N_PIECES):
-                piece_offsets = offsets[:, j * OFFSET_COLS : (j + 1) * OFFSET_COLS]
-                gate = work.tile([P, PIECE], F32, name="gate")
-                nc.scalar.activation(gate[:], tables[k][:].indirect(piece_offsets), RELU)
-                x = work.tile([P, PIECE], BF16, name="x")
-                nc.vector.tensor_tensor(x[:], gate[:], streams[k, j][:], MULT)
-                xs[k, j] = x
+        for k, j in order:
+            piece_offsets = offsets[:, j * OFFSET_COLS : (j + 1) * OFFSET_COLS]
+            gate = work.tile([P, PIECE], F32, name="gate")
+            nc.scalar.activation(gate[:], tables[k][:].indirect(piece_offsets), RELU)
+            x = work.tile([P, PIECE], BF16, name="x")
+            nc.vector.tensor_tensor(x[:], gate[:], streams[k, j][:], MULT)
+            xs[k, j] = x
 
         for j in range(N_PIECES):
             for m in range(M_BLOCKS):

import concourse.mybir as mybir

F32 = mybir.dt.float32
BF16 = mybir.dt.bfloat16
U16 = mybir.dt.uint16
RELU = mybir.ActivationFunctionType.Relu
ADD = mybir.AluOpType.add
MAX = mybir.AluOpType.max
MULT = mybir.AluOpType.mult

P = 128
K_ROWS = 256
M_ROWS = 256
TABLE_COLS = 2048
N = 1536
PIECE = 512
GROUP = 2
K_BLOCKS = K_ROWS // P
M_BLOCKS = M_ROWS // P
N_PIECES = N // PIECE
OFFSET_COLS = PIECE // 16

FLOPS = 2 * K_ROWS * M_ROWS * N


def tile_lookup_gate_relu_relu_kernel(tc, tab, y, w, b, offs, out):
    nc = tc.nc
    order = []
    for first in range(0, N_PIECES, GROUP):
        for k in range(K_BLOCKS):
            for j in range(first, min(first + GROUP, N_PIECES)):
                order.append((k, j))
    with (
        tc.tile_pool(name="held", bufs=1) as held,
        tc.tile_pool(name="work", bufs=K_BLOCKS * N_PIECES) as work,
        tc.psum_pool(name="psum", bufs=M_BLOCKS * N_PIECES) as psum,
    ):
        zero = held.tile([P, 1], F32, name="zero")
        nc.vector.memset(zero[:], 0.0)
        warm = held.tile([P, 1], F32, name="warm")
        nc.scalar.activation(warm[:], zero[:], RELU)

        offsets = held.tile([P, N // 16], U16, name="offsets")
        nc.sync.dma_start(offsets[:], offs)
        tables = []
        for k in range(K_BLOCKS):
            table = held.tile([P, TABLE_COLS], F32, name=f"table{k}")
            nc.sync.dma_start(table[:], tab[k * P : (k + 1) * P, :])
            tables.append(table)
        weights = held.tile([P, K_BLOCKS, M_ROWS], BF16, name="weights")
        nc.sync.dma_start(weights[:], w.rearrange("(k p) m -> p k m", p=P))
        biases = []
        for m in range(M_BLOCKS):
            bias = held.tile([P, 1], F32, name=f"bias{m}")
            nc.sync.dma_start(bias[:], b[m * P : (m + 1) * P, :])
            biases.append(bias)
        streams = {}
        for k, j in order:
            stream = held.tile([P, PIECE], F32, name=f"stream{k}_{j}")
            nc.sync.dma_start(stream[:], y[k * P : (k + 1) * P, j * PIECE : (j + 1) * PIECE])
            streams[k, j] = stream

        xs = {}
        for k, j in order:
            piece_offsets = offsets[:, j * OFFSET_COLS : (j + 1) * OFFSET_COLS]
            gate = work.tile([P, PIECE], F32, name="gate")
            nc.scalar.activation(gate[:], tables[k][:].indirect(piece_offsets), RELU)
            x = work.tile([P, PIECE], BF16, name="x")
            nc.vector.tensor_tensor(x[:], gate[:], streams[k, j][:], MULT)
            xs[k, j] = x

        for j in range(N_PIECES):
            for m in range(M_BLOCKS):
                acc = psum.tile([P, PIECE], F32, name="acc")
                for k in range(K_BLOCKS):
                    nc.tensor.matmul(
                        acc[:],
                        weights[:, k, m * P : (m + 1) * P],
                        xs[k, j][:],
                        start=k == 0,
                        stop=k == K_BLOCKS - 1,
                    )
                result = work.tile([P, PIECE], F32, name="result")
                if m % 2 == 0:
                    nc.vector.tensor_scalar(result[:], acc[:], biases[m][:], 0.0, ADD, MAX)
                else:
                    nc.scalar.activation(result[:], acc[:], RELU, bias=biases[m][:])
                nc.sync.dma_start(out[m * P : (m + 1) * P, j * PIECE : (j + 1) * PIECE], result[:])
